import numpy as np, ml_dtypes
CORES = [0,1,2,3,4,5,6,7,8,9,10,11,12,13,14,15]
N = 16
ROOT = 15
def setup_inputs(rng):
    return {"x": rng.standard_normal((N, 128, 512), dtype=np.float32).astype(ml_dtypes.bfloat16)}
def reference(x):
    y = np.full((N, 128, N * 512), np.nan, x.dtype)
    y[ROOT] = np.concatenate(list(x), axis=1)
    return {"y": y}

@@ -1,0 +1,53 @@
+B = 512
+ROOT = 15
+
+SCRATCH = {
+    "xs": ("sbuf", [128, B], "bfloat16"),
+    "rel": ("sbuf", [128, B], "bfloat16"),
+    "land": ("sbuf", [128, 16 * B], "bfloat16"),
+}
+SEMAPHORES = ["loaded", "sent", "handed", "near", "wave1", "wave2", "stored"]
+
+
+def rank_program(g, core, T, topo):
+    s = T.sem
+
+    def cols(t, a, b):
+        return t[:, a * B:b * B]
+
+    def send(dst, out_ap, in_ap, remote_sem):
+        rid, pid, _se = topo.addr(dst)
+        g.remote_dma(out_ap, in_ap, remote_sem, s.sent, pid, rid, topo.mask(core, dst))
+
+    if core == ROOT:
+        n = 0
+        g.dma_start(cols(T.y, ROOT, ROOT + 1), T.x[:]).then_inc(s.stored, 16)
+        n += 16
+        g.wait_ge(s.near, 7 * 16)
+        g.dma_start(cols(T.y, 8, 15), cols(T.land, 8, 15)).then_inc(s.stored, 16)
+        n += 16
+        g.wait_ge(s.wave1, 4 * 8)
+        for a in (2, 6):
+            g.dma_start(cols(T.y, a, a + 2), cols(T.land, a, a + 2)).then_inc(s.stored, 16)
+            n += 16
+        g.wait_ge(s.wave2, 4 * 8)
+        for a in (0, 4):
+            g.dma_start(cols(T.y, a, a + 2), cols(T.land, a, a + 2)).then_inc(s.stored, 16)
+            n += 16
+        g.wait_ge(s.stored, n)
+        return
+
+    g.dma_start(T.xs[:], T.x[:]).then_inc(s.loaded, 16)
+    g.wait_ge(s.loaded, 16)
+
+    if topo.chip(core) == topo.chip(ROOT):
+        send(ROOT, cols(T.land, core, core + 1), T.xs[:], s.near)
+        g.wait_ge(s.sent, 16)
+    elif topo.may_write(core, ROOT):
+        send(ROOT, cols(T.land, core, core + 1), T.xs[:], s.wave1)
+        g.wait_ge(s.handed, 16)
+        send(ROOT, cols(T.land, core - 2, core - 1), T.rel[:], s.wave2)
+        g.wait_ge(s.sent, 16)
+    else:
+        send(core + 2, T.rel[:], T.xs[:], s.handed)
+        g.wait_ge(s.sent, 16)

@@ -1,12 +1,14 @@
 B = 512
 ROOT = 15
+HAND = {0: (2, 0), 4: (2, 1), 1: (6, 0), 5: (6, 1)}
 
 SCRATCH = {
     "xs": ("sbuf", [128, B], "bfloat16"),
-    "rel": ("sbuf", [128, B], "bfloat16"),
+    "rel0": ("sbuf", [128, B], "bfloat16"),
+    "rel1": ("sbuf", [128, B], "bfloat16"),
     "land": ("sbuf", [128, 16 * B], "bfloat16"),
 }
-SEMAPHORES = ["loaded", "sent", "handed", "near", "wave1", "wave2", "stored"]
+SEMAPHORES = ["loaded", "sent", "handed0", "handed1", "near", "wave1", "wave2", "wave3", "stored"]
 
 
 def rank_program(g, core, T, topo):
@@ -20,20 +22,18 @@ def rank_program(g, core, T, topo):
         g.remote_dma(out_ap, in_ap, remote_sem, s.sent, pid, rid, topo.mask(core, dst))
 
     if core == ROOT:
-        n = 0
         g.dma_start(cols(T.y, ROOT, ROOT + 1), T.x[:]).then_inc(s.stored, 16)
-        n += 16
-        g.wait_ge(s.near, 7 * 16)
-        g.dma_start(cols(T.y, 8, 15), cols(T.land, 8, 15)).then_inc(s.stored, 16)
-        n += 16
-        g.wait_ge(s.wave1, 4 * 8)
-        for a in (2, 6):
-            g.dma_start(cols(T.y, a, a + 2), cols(T.land, a, a + 2)).then_inc(s.stored, 16)
-            n += 16
-        g.wait_ge(s.wave2, 4 * 8)
-        for a in (0, 4):
-            g.dma_start(cols(T.y, a, a + 2), cols(T.land, a, a + 2)).then_inc(s.stored, 16)
-            n += 16
+        n = 16
+        for sem, count, groups in (
+            (s.near, 7 * 16, ((8, 15),)),
+            (s.wave1, 4 * 8, ((2, 4), (6, 8))),
+            (s.wave2, 2 * 8, ((0, 2),)),
+            (s.wave3, 2 * 8, ((4, 6),)),
+        ):
+            g.wait_ge(sem, count)
+            for a, b in groups:
+                g.dma_start(cols(T.y, a, b), cols(T.land, a, b)).then_inc(s.stored, 16)
+                n += 16
         g.wait_ge(s.stored, n)
         return
 
@@ -43,11 +43,17 @@ def rank_program(g, core, T, topo):
     if topo.chip(core) == topo.chip(ROOT):
         send(ROOT, cols(T.land, core, core + 1), T.xs[:], s.near)
         g.wait_ge(s.sent, 16)
-    elif topo.may_write(core, ROOT):
-        send(ROOT, cols(T.land, core, core + 1), T.xs[:], s.wave1)
-        g.wait_ge(s.handed, 16)
-        send(ROOT, cols(T.land, core - 2, core - 1), T.rel[:], s.wave2)
+    elif core in HAND:
+        gw, slot = HAND[core]
+        send(gw, (T.rel0, T.rel1)[slot][:], T.xs[:], (s.handed0, s.handed1)[slot])
         g.wait_ge(s.sent, 16)
     else:
-        send(core + 2, T.rel[:], T.xs[:], s.handed)
-        g.wait_ge(s.sent, 16)
+        send(ROOT, cols(T.land, core, core + 1), T.xs[:], s.wave1)
+        n = 8
+        for slot in (0, 1):
+            for h in sorted(HAND):
+                if HAND[h] == (core, slot):
+                    g.wait_ge((s.handed0, s.handed1)[slot], 16)
+                    send(ROOT, cols(T.land, h, h + 1), (T.rel0, T.rel1)[slot][:], (s.wave2, s.wave3)[slot])
+                    n += 8
+        g.wait_ge(s.sent, n)

@@ -1,18 +1,25 @@
+from concourse.bass import DstId, RemoteDMATransfer
+
 B = 512
+H = B // 2
 ROOT = 15
-HAND = {0: (2, 0), 4: (2, 1), 1: (6, 0), 5: (6, 1)}
+HAND = {0: (2, 6, 0), 1: (3, 7, 0), 4: (2, 6, 1), 5: (2, 6, 2)}
 
 SCRATCH = {
     "xs": ("sbuf", [128, B], "bfloat16"),
-    "rel0": ("sbuf", [128, B], "bfloat16"),
-    "rel1": ("sbuf", [128, B], "bfloat16"),
+    "rel0": ("sbuf", [128, H], "bfloat16"),
+    "rel1": ("sbuf", [128, H], "bfloat16"),
+    "rel2": ("sbuf", [128, H], "bfloat16"),
     "land": ("sbuf", [128, 16 * B], "bfloat16"),
 }
-SEMAPHORES = ["loaded", "sent", "handed0", "handed1", "near", "wave1", "wave2", "wave3", "stored"]
+SEMAPHORES = ["loaded", "loaded2", "sent", "handed0", "handed1", "handed2",
+              "near", "g67", "g0123", "g4", "g5", "stored"]
 
 
 def rank_program(g, core, T, topo):
     s = T.sem
+    rel = (T.rel0, T.rel1, T.rel2)
+    handed = (s.handed0, s.handed1, s.handed2)
 
     def cols(t, a, b):
         return t[:, a * B:b * B]
@@ -24,36 +31,52 @@ def rank_program(g, core, T, topo):
     if core == ROOT:
         g.dma_start(cols(T.y, ROOT, ROOT + 1), T.x[:]).then_inc(s.stored, 16)
         n = 16
-        for sem, count, groups in (
-            (s.near, 7 * 16, ((8, 15),)),
-            (s.wave1, 4 * 8, ((2, 4), (6, 8))),
-            (s.wave2, 2 * 8, ((0, 2),)),
-            (s.wave3, 2 * 8, ((4, 6),)),
+        for sem, count, a, b in (
+            (s.near, 7 * 16, 8, 15),
+            (s.g67, 4 * 8, 6, 8),
+            (s.g0123, 8 * 8, 0, 4),
+            (s.g4, 2 * 8, 4, 5),
+            (s.g5, 2 * 8, 5, 6),
         ):
             g.wait_ge(sem, count)
-            for a, b in groups:
-                g.dma_start(cols(T.y, a, b), cols(T.land, a, b)).then_inc(s.stored, 16)
-                n += 16
+            g.dma_start(cols(T.y, a, b), cols(T.land, a, b)).then_inc(s.stored, 16)
+            n += 16
         g.wait_ge(s.stored, n)
         return
 
-    g.dma_start(T.xs[:], T.x[:]).then_inc(s.loaded, 16)
-    g.wait_ge(s.loaded, 16)
-
     if topo.chip(core) == topo.chip(ROOT):
+        g.dma_start(T.xs[:], T.x[:]).then_inc(s.loaded, 16)
+        g.wait_ge(s.loaded, 16)
         send(ROOT, cols(T.land, core, core + 1), T.xs[:], s.near)
         g.wait_ge(s.sent, 16)
     elif core in HAND:
-        gw, slot = HAND[core]
-        send(gw, (T.rel0, T.rel1)[slot][:], T.xs[:], (s.handed0, s.handed1)[slot])
+        g.dma_start(T.xs[:], T.x[:]).then_inc(s.loaded, 16)
+        g.wait_ge(s.loaded, 16)
+        slot = HAND[core][2]
+        trs = []
+        for k in (0, 1):
+            rid, pid, _se = topo.addr(HAND[core][k])
+            trs.append(RemoteDMATransfer(
+                dst_ids=[DstId(rid=rid, pnc=pid)], dma_engine_mask=0x00FF << (8 * k), remote_sem=handed[slot],
+                src=T.xs[:, k * H:(k + 1) * H], dst=rel[slot][:]))
+        g.remote_dma_fused(trs, local_sem=s.sent)
         g.wait_ge(s.sent, 16)
     else:
-        send(ROOT, cols(T.land, core, core + 1), T.xs[:], s.wave1)
-        n = 8
-        for slot in (0, 1):
+        own = s.g67 if core >= 6 else s.g0123
+        for k, sem in ((0, s.loaded), (1, s.loaded2)):
+            g.dma_start(T.xs[:, k * H:(k + 1) * H], T.x[:, k * H:(k + 1) * H]).then_inc(sem, 16)
+        n = 0
+        for k, sem in ((0, s.loaded), (1, s.loaded2)):
+            g.wait_ge(sem, 16)
+            c0 = core * B + k * H
+            send(ROOT, T.land[:, c0:c0 + H], T.xs[:, k * H:(k + 1) * H], own)
+            n += 8
+        group = {0: s.g0123, 1: s.g0123, 4: s.g4, 5: s.g5}
+        for slot in (0, 1, 2):
             for h in sorted(HAND):
-                if HAND[h] == (core, slot):
-                    g.wait_ge((s.handed0, s.handed1)[slot], 16)
-                    send(ROOT, cols(T.land, h, h + 1), (T.rel0, T.rel1)[slot][:], (s.wave2, s.wave3)[slot])
+                if HAND[h][2] == slot and core in HAND[h][:2]:
+                    c0 = h * B + HAND[h][:2].index(core) * H
+                    g.wait_ge(handed[slot], 8)
+                    send(ROOT, T.land[:, c0:c0 + H], rel[slot][:], group[h])
                     n += 8
         g.wait_ge(s.sent, n)

from concourse.bass import DstId, RemoteDMATransfer

B = 512
H = B // 2
ROOT = 15
HAND = {0: (2, 6, 0), 1: (3, 7, 0), 4: (2, 6, 1), 5: (2, 6, 2)}

SCRATCH = {
    "xs": ("sbuf", [128, B], "bfloat16"),
    "rel0": ("sbuf", [128, H], "bfloat16"),
    "rel1": ("sbuf", [128, H], "bfloat16"),
    "rel2": ("sbuf", [128, H], "bfloat16"),
    "land": ("sbuf", [128, 16 * B], "bfloat16"),
}
SEMAPHORES = ["loaded", "loaded2", "sent", "handed0", "handed1", "handed2",
              "near", "g67", "g0123", "g4", "g5", "stored"]


def rank_program(g, core, T, topo):
    s = T.sem
    rel = (T.rel0, T.rel1, T.rel2)
    handed = (s.handed0, s.handed1, s.handed2)

    def cols(t, a, b):
        return t[:, a * B:b * B]

    def send(dst, out_ap, in_ap, remote_sem):
        rid, pid, _se = topo.addr(dst)
        g.remote_dma(out_ap, in_ap, remote_sem, s.sent, pid, rid, topo.mask(core, dst))

    if core == ROOT:
        g.dma_start(cols(T.y, ROOT, ROOT + 1), T.x[:]).then_inc(s.stored, 16)
        n = 16
        for sem, count, a, b in (
            (s.near, 7 * 16, 8, 15),
            (s.g67, 4 * 8, 6, 8),
            (s.g0123, 8 * 8, 0, 4),
            (s.g4, 2 * 8, 4, 5),
            (s.g5, 2 * 8, 5, 6),
        ):
            g.wait_ge(sem, count)
            g.dma_start(cols(T.y, a, b), cols(T.land, a, b)).then_inc(s.stored, 16)
            n += 16
        g.wait_ge(s.stored, n)
        return

    if topo.chip(core) == topo.chip(ROOT):
        g.dma_start(T.xs[:], T.x[:]).then_inc(s.loaded, 16)
        g.wait_ge(s.loaded, 16)
        send(ROOT, cols(T.land, core, core + 1), T.xs[:], s.near)
        g.wait_ge(s.sent, 16)
    elif core in HAND:
        g.dma_start(T.xs[:], T.x[:]).then_inc(s.loaded, 16)
        g.wait_ge(s.loaded, 16)
        slot = HAND[core][2]
        trs = []
        for k in (0, 1):
            rid, pid, _se = topo.addr(HAND[core][k])
            trs.append(RemoteDMATransfer(
                dst_ids=[DstId(rid=rid, pnc=pid)], dma_engine_mask=0x00FF << (8 * k), remote_sem=handed[slot],
                src=T.xs[:, k * H:(k + 1) * H], dst=rel[slot][:]))
        g.remote_dma_fused(trs, local_sem=s.sent)
        g.wait_ge(s.sent, 16)
    else:
        own = s.g67 if core >= 6 else s.g0123
        for k, sem in ((0, s.loaded), (1, s.loaded2)):
            g.dma_start(T.xs[:, k * H:(k + 1) * H], T.x[:, k * H:(k + 1) * H]).then_inc(sem, 16)
        n = 0
        for k, sem in ((0, s.loaded), (1, s.loaded2)):
            g.wait_ge(sem, 16)
            c0 = core * B + k * H
            send(ROOT, T.land[:, c0:c0 + H], T.xs[:, k * H:(k + 1) * H], own)
            n += 8
        group = {0: s.g0123, 1: s.g0123, 4: s.g4, 5: s.g5}
        for slot in (0, 1, 2):
            for h in sorted(HAND):
                if HAND[h][2] == slot and core in HAND[h][:2]:
                    c0 = h * B + HAND[h][:2].index(core) * H
                    g.wait_ge(handed[slot], 8)
                    send(ROOT, T.land[:, c0:c0 + H], rel[slot][:], group[h])
                    n += 8
        g.wait_ge(s.sent, n)
